import numpy as np
import ml_dtypes


def mxq(x, axis, fmt="e4m3"):
    dtype, down = {"e4m3": (ml_dtypes.float8_e4m3fn, 7), "e5m2": (ml_dtypes.float8_e5m2, 14)}[fmt]
    v = np.moveaxis(np.asarray(x, np.float32).astype(ml_dtypes.bfloat16).astype(np.float64), axis, -1)
    blocks = v.reshape(v.shape[:-1] + (-1, 32))
    amax = np.abs(blocks).max(-1, keepdims=True)
    byte = np.maximum(np.where(amax > 0, np.frexp(amax)[1] - 1 + 127, 0) - down, 1)
    scale = np.exp2(byte - 127.0)
    codes = (blocks / scale).astype(np.float32).astype(dtype).astype(np.float64)
    return np.moveaxis((codes * scale).reshape(v.shape), -1, axis)


WIDE = False


def mx_kscale(k):
    if not WIDE:
        return np.ones(k)
    levels = np.array([10, -10, 5, -5, 0])
    if k % 512:
        return np.exp2(np.random.permutation(np.resize(levels, k // 32))).repeat(32)
    a = np.empty((k // 512, 16))
    for p in range(k // 512):
        a[p, :8] = np.random.permutation(np.resize(levels, 8))
        for g in range(8):
            far = levels[np.abs(levels - a[p, g]) >= 10]
            a[p, g + 8] = far[np.random.randint(len(far))]
    return np.exp2(a.ravel()).repeat(32)


def f64(x):
    return np.asarray(x).astype(np.float64)


def striped8(idx):
    return np.concatenate([x.reshape(-1, 16).T for x in idx]).astype(np.uint16)


def runs(offs, k):
    lists = np.stack([offs[16 * r : 16 * r + 16].T.reshape(-1) for r in range(8)]).astype(np.int64)
    return lists[np.arange(k) % 512 // 64]


def pack_weight(w):
    k, n = w.shape
    w = f64(np.asarray(w, np.float32).astype(ml_dtypes.bfloat16)).reshape(k // 32, 32, n)
    amax = np.abs(w).max(1)
    byte = np.clip(np.where(amax > 0, np.frexp(amax)[1] - 1 + 127 - 7, 1), 1, 254)
    scaled = (w * np.exp2(127.0 - byte)[:, None, :]).reshape(k, n).astype(np.float32)
    words = np.ascontiguousarray(scaled.reshape(k // 512, 128, 4, n).transpose(0, 1, 3, 2)).astype(ml_dtypes.float8_e4m3fn).view(np.uint8)
    return words, np.ascontiguousarray(byte.astype(np.uint8).reshape(k // 512, 16, n))


def unpack_weight(words, scales):
    g, p, n, _ = words.shape
    vals = np.ascontiguousarray(words).view(ml_dtypes.float8_e4m3fn).astype(np.float64) * np.repeat(np.exp2(scales.astype(np.float64) - 127.0), 8, axis=1)[..., None]
    return vals.transpose(0, 1, 3, 2).reshape(g * 512, n)


K, T, S, H, C = 512, 2048, 512, 512, 512


def setup_inputs():
    n = np.random.standard_normal
    s = mx_kscale(K)[:, None]
    packed_xT = pack_weight(n((K, T)) * s)
    return {
        "x_words": packed_xT[0],
        "x_scales": packed_xT[1],
        "w1": (n((K, H)) / np.sqrt(K) / s).astype(np.float32),
        "gs": (np.random.uniform(0.5, 1.5, (K, 1)) / s).astype(np.float32),
        "offs": striped8(np.random.randint(0, T, (8, S))),
        "n1": striped8(np.stack([np.random.permutation(S) for _ in range(8)])),
        "n2": striped8(np.stack([np.random.permutation(S) for _ in range(8)])),
        "cand": striped8(np.random.randint(0, T, (8, C))),
        "n3": striped8(np.stack([np.random.permutation(S) for _ in range(8)])),
        "n4": striped8(np.stack([np.random.permutation(S) for _ in range(8)])),
    }


def reference(x_words, x_scales, w1, gs, offs, n1, n2, cand, n3, n4):
    x_cand = unpack_weight(x_words, x_scales)[np.arange(K)[:, None], runs(cand, K)]
    xq = unpack_weight(x_words, x_scales)[np.arange(K)[:, None], runs(offs, K)]
    y = mxq(f64(w1), 0, "e4m3").T @ xq
    pa = y[np.arange(H)[:, None], runs(n1, H)]
    pb = y[np.arange(H)[:, None], runs(n2, H)]
    z = f64(gs) * (np.maximum(np.maximum(y, pa), pb) - (0.5 * (np.minimum(np.minimum(y, pa), pb))))
    s = 0.0625 * ((x_cand.T @ mxq(z, 0, "e4m3")))
    st = np.maximum(s, s[np.arange(C)[:, None], runs(n3, C)])
    return np.minimum(st, st[np.arange(C)[:, None], runs(n4, C)])

@@ -1,0 +1,293 @@
+from contextlib import ExitStack
+
+import concourse.mybir as mybir
+from concourse.masks import make_identity
+
+K, T, S, H, C = 512, 2048, 512, 512, 512
+FLOPS = 2 * K * H * S + 2 * K * C * S
+
+F32 = mybir.dt.float32
+BF16 = mybir.dt.bfloat16
+I32 = mybir.dt.int32
+U32 = mybir.dt.uint32
+U16 = mybir.dt.uint16
+U8 = mybir.dt.uint8
+FP8X4 = mybir.dt.float8_e4m3fn_x4
+ALU = mybir.AluOpType
+ACT = mybir.ActivationFunctionType
+
+P = 128
+PACK = 4
+BLK = 128
+NBLK = S // BLK
+PE_BLKS = NBLK - 1
+PE_COLS = PE_BLKS * BLK
+WIDE = 2 * S
+PER_COL = 16
+W_VEC = 44
+
+
+def tile_picked_hcandrangehopmn_none_p_kernel(
+    tc, x_words, x_scales, w1, gs, offs, n1, n2, cand, n3, n4, out
+):
+    nc = tc.nc
+    with ExitStack() as ctx:
+        keep = ctx.enter_context(tc.tile_pool(name="keep", bufs=1))
+        ring = ctx.enter_context(tc.tile_pool(name="ring", bufs=2))
+        psum = ctx.enter_context(tc.psum_pool(name="psum", bufs=1))
+
+        def list_tile(name):
+            return keep.tile([P, S // PER_COL], U16, name=name)
+
+        offs_l, cand_l = list_tile("offs_l"), list_tile("cand_l")
+        n1_l, n2_l, n3_l, n4_l = (list_tile(n) for n in ("n1_l", "n2_l", "n3_l", "n4_l"))
+
+        table_bytes = keep.tile([P, T], U8, name="table_bytes", align_bytes=64)
+        table_words = keep.tile([P, T], I32, name="table_words", align_bytes=64)
+        gs_t = keep.tile([P, PACK], F32, name="gs_t")
+        w_raw = [keep.tile([P, PACK, H // 2], F32, name=f"w_raw{h}", align_bytes=64) for h in range(2)]
+
+        nc.sync.dma_start(
+            table_bytes[:].bitcast(I32), x_scales[0].bitcast(I32).unsqueeze(1).to_broadcast([16, 8, T // 4])
+        )
+        nc.sync.dma_start(offs_l[:], offs)
+        nc.sync.dma_start(gs_t[:], gs.rearrange("(p t) o -> p (t o)", t=PACK))
+        nc.sync.dma_start(cand_l[:], cand)
+        nc.sync.dma_start(table_words[:], x_words[0].rearrange("p c r -> p (c r)").bitcast(I32))
+        nc.sync.dma_start(n1_l[:], n1)
+        nc.sync.dma_start(n2_l[:], n2)
+        w_rows = w1.rearrange("(p j) c -> p j c", j=PACK)
+        for h in range(2):
+            nc.sync.dma_start(w_raw[h][:], w_rows[:, :, h * (H // 2) : (h + 1) * (H // 2)])
+        nc.sync.dma_start(n3_l[:], n3)
+        nc.sync.dma_start(n4_l[:], n4)
+
+        sign = keep.tile([P, PACK], F32, name="sign")
+        alpha = keep.tile([P, PACK], F32, name="alpha")
+        beta = keep.tile([P, PACK], F32, name="beta")
+        nc.scalar.activation(sign[:], gs_t[:], ACT.Sign)
+        nc.scalar.activation(alpha[:], sign[:], ACT.Copy, scale=1.5, bias=0.5)
+        nc.scalar.activation(beta[:], sign[:], ACT.Copy, scale=-1.5, bias=0.5)
+
+        x_plane = keep.tile([P, S], U8, name="x_plane", align_bytes=64)
+        c_plane = keep.tile([P, C], U8, name="c_plane", align_bytes=64)
+        ident = keep.tile([P, P], F32, name="ident")
+        wide_a = [keep.tile([P, WIDE], F32, name=f"wide_a{t}") for t in range(PACK)]
+        wide_st = [keep.tile([P, WIDE], F32, name=f"wide_st{t}") for t in range(PACK)]
+        nc.gpsimd.memset(x_plane[:].bitcast(I32), 0)
+        nc.gpsimd.memset(c_plane[:].bitcast(I32), 0)
+        for t in range(PACK):
+            nc.vector.memset(wide_a[t][:, S:], 0.0)
+        make_identity(nc, ident[:])
+        for t in range(PACK):
+            nc.gpsimd.memset(wide_st[t][:, S:], 0.0)
+
+        def place_scale_rows(queue, plane, picked):
+            for b in range(4):
+                queue.dma_start(plane[b:P:32, :].bitcast(I32), picked[8 * b : P : 32, :].bitcast(I32))
+
+        x_bytes = keep.tile([P, S], U8, name="x_bytes", align_bytes=64)
+        nc.vector.tensor_copy(x_bytes[:], table_bytes[:].indirect(offs_l[:]))
+        place_scale_rows(nc.scalar, x_plane, x_bytes)
+
+        c_bytes = keep.tile([P, C], U8, name="c_bytes", align_bytes=64)
+        nc.vector.tensor_copy(c_bytes[:], table_bytes[:].indirect(cand_l[:]))
+
+        x_codes = keep.tile([P, S], U32, name="x_codes", align_bytes=64)
+        nc.vector.tensor_copy(x_codes[:], table_words[:].bitcast(U32).indirect(offs_l[:]))
+
+        c_words = keep.tile([P, C], U32, name="c_words", align_bytes=64)
+        nc.vector.tensor_copy(c_words[:], table_words[:].bitcast(U32).indirect(cand_l[:]))
+
+        w_bf = keep.tile([P, PACK * H], BF16, name="w_bf", align_bytes=64)
+        w_codes = keep.tile([P, H], U32, name="w_codes", align_bytes=64)
+        w_plane = keep.tile([P, H], U8, name="w_plane", align_bytes=64)
+        w_dst = w_bf[:].rearrange("p (t m j) -> p m j t", t=PACK, j=PACK)
+        half = P // 2
+        nc.scalar.activation(w_dst[:, 0:half], w_raw[0][:].rearrange("p j (m t) -> p m j t", t=PACK), ACT.Copy)
+        w_late = w_raw[1][:].rearrange("p j (m t) -> p m j t", t=PACK)
+        nc.vector.tensor_copy(w_dst[:, half : half + W_VEC], w_late[:, 0:W_VEC])
+        nc.scalar.activation(w_dst[:, half + W_VEC : P], w_late[:, W_VEC:half], ACT.Copy)
+
+        y_b = [keep.tile([P, S], F32, name=f"y_b{t}") for t in range(PACK)]
+        for t in range(PACK):
+            cols = slice(t * P, (t + 1) * P)
+            nc.vector.quantize_mx(
+                out=w_codes[:, cols].bitcast(FP8X4),
+                scales=w_plane[:, cols],
+                in_=w_bf[:, t * PACK * P : (t + 1) * PACK * P],
+            )
+            parts = [(0, S // 2, "acc0"), (S // 2, S, "acc_spare")] if t == 0 else [(0, S, f"acc{t}")]
+            for lo_c, hi_c, bank in parts:
+                acc = psum.tile([P, hi_c - lo_c], F32, name=bank)
+                nc.tensor.matmul_mx(
+                    out=acc[:],
+                    lhsT=w_codes[:, cols].bitcast(FP8X4),
+                    lhsT_scale=w_plane[:, cols],
+                    rhs=x_codes[:, lo_c:hi_c].bitcast(FP8X4),
+                    rhs_scale=x_plane[:, lo_c:hi_c],
+                    start=True,
+                    stop=True,
+                )
+                for dst in (wide_a[t], y_b[t]):
+                    if lo_c == 0:
+                        nc.scalar.activation(dst[:, lo_c:hi_c], acc[:], ACT.Copy, scale=gs_t[:, t : t + 1])
+                    else:
+                        nc.vector.tensor_scalar(dst[:, lo_c:hi_c], acc[:], gs_t[:, t : t + 1], None, ALU.mult)
+
+        c_bytes_dealt = keep.tile([P, C], U8, name="w_raw1", align_bytes=64)
+        nc.vector.tensor_copy(
+            c_bytes_dealt[:].rearrange("p (t m) -> p m t", t=PACK), c_bytes[:].rearrange("p (m t) -> p m t", t=PACK)
+        )
+        place_scale_rows(nc.sync, c_plane, c_bytes_dealt)
+        c_codes = keep.tile([P, C], U32, name="w_bf", align_bytes=64)
+        nc.vector.tensor_copy(
+            c_codes[:].rearrange("p (t m) -> p m t", t=PACK), c_words[:].rearrange("p (m t) -> p m t", t=PACK)
+        )
+
+        lead = slice(0, PE_COLS // PER_COL)
+        last = slice(PE_COLS // PER_COL, S // PER_COL)
+        sums = [psum.tile([P, PACK, P], F32, name=f"turn{b}") for b in range(PE_BLKS)]
+        z_turned = [keep.tile([P, 2, P, 2], BF16, name=f"z_turned{b}", align_bytes=64) for b in range(PE_BLKS)]
+        d1, d2 = {}, {}
+
+        def diff(dst, t, lst):
+            nc.vector.tensor_tensor(dst[:], wide_a[t][:].indirect(lst[:, lead]), y_b[t][:, 0:PE_COLS], ALU.subtract)
+
+        def first(t):
+            d1[t] = ring.tile([P, PE_COLS], F32, name="d1")
+            diff(d1[t], t, n1_l)
+
+        def second(t):
+            d2[t] = ring.tile([P, PE_COLS], F32, name="d2")
+            diff(d2[t], t, n2_l)
+
+        def combine(t):
+            hi = ring.tile([P, PE_COLS], F32, name="hi")
+            lo = ring.tile([P, PE_COLS], F32, name="lo")
+            nc.vector.scalar_tensor_tensor(hi[:], d1[t][:], 0.0, d2[t][:], ALU.max, ALU.max)
+            nc.vector.scalar_tensor_tensor(lo[:], d1[t][:], 0.0, d2[t][:], ALU.min, ALU.min)
+            hi_w = ring.tile([P, PE_COLS], F32, name="hi_w")
+            lo_w = ring.tile([P, PE_COLS], F32, name="lo_w")
+            nc.scalar.activation(hi_w[:], hi[:], ACT.Copy, scale=alpha[:, t : t + 1])
+            nc.scalar.activation(lo_w[:], lo[:], ACT.Copy, scale=beta[:, t : t + 1])
+            for b in range(PE_BLKS):
+                cols = slice(b * BLK, (b + 1) * BLK)
+                for i, term in enumerate((y_b[t], hi_w, lo_w)):
+                    nc.tensor.matmul(
+                        sums[b][:, t, :], lhsT=term[:, cols], rhs=ident[:], is_transpose=True, start=(i == 0), stop=(i == 2)
+                    )
+            if t % 2 == 1:
+                u = t // 2
+                for b in range(PE_BLKS):
+                    nc.scalar.activation(
+                        z_turned[b][:, u], sums[b][:, 2 * u : 2 * u + 2, :].rearrange("j e p -> j p e"), ACT.Copy, scale=0.5
+                    )
+
+        first(0)
+        for t in range(PACK):
+            second(t)
+            if t + 1 < PACK:
+                first(t + 1)
+            else:
+                e1 = keep.tile([P, PACK, BLK], F32, name="e1")
+                nc.vector.tensor_tensor(e1[:, 0, :], y_b[0][:].indirect(n1_l[:, last]), wide_a[0][:, PE_COLS:S], ALU.subtract)
+            combine(t)
+
+        z_bf = [keep.tile([P, BLK * PACK], BF16, name=f"z_bf{b}", align_bytes=64) for b in range(NBLK)]
+        z_codes = [keep.tile([P, BLK], U32, name=f"z_codes{b}", align_bytes=64) for b in range(NBLK)]
+        z_plane = [keep.tile([P, BLK], U8, name=f"z_plane{b}", align_bytes=64) for b in range(NBLK)]
+        for b in range(PE_BLKS):
+            back = psum.tile([P, 2, BLK], F32, name=f"turn{b}")
+            words = z_turned[b][:].rearrange("j u p e -> j (u p e)").bitcast(F32)
+            for u in range(2):
+                nc.tensor.transpose(back[:, u, :], words[:, u * P : (u + 1) * P], ident[:])
+            nc.scalar.copy(z_bf[b][:].bitcast(F32).rearrange("p (j u) -> p j u", u=2), back[:].rearrange("p u j -> p j u"))
+
+        scores = [psum.tile([P, S], F32, name=f"acc{t}") for t in range(PACK)]
+
+        def quantize_and_score(b):
+            nc.vector.quantize_mx(out=z_codes[b][:].bitcast(FP8X4), scales=z_plane[b][:], in_=z_bf[b][:])
+            for t in range(PACK):
+                cols = slice(t * P, (t + 1) * P)
+                nc.tensor.matmul_mx(
+                    out=scores[t][:, b * BLK : (b + 1) * BLK],
+                    lhsT=c_codes[:, cols].bitcast(FP8X4),
+                    lhsT_scale=c_plane[:, cols],
+                    rhs=z_codes[b][:].bitcast(FP8X4),
+                    rhs_scale=z_plane[b][:],
+                    start=True,
+                    stop=True,
+                )
+
+        e2 = keep.tile([P, PACK, BLK], F32, name="e2")
+        for t in range(PACK):
+            if t > 0:
+                nc.vector.tensor_tensor(e1[:, t, :], y_b[t][:].indirect(n1_l[:, last]), wide_a[t][:, PE_COLS:S], ALU.subtract)
+            nc.vector.tensor_tensor(e2[:, t, :], y_b[t][:].indirect(n2_l[:, last]), wide_a[t][:, PE_COLS:S], ALU.subtract)
+        hi_l = keep.tile([P, PACK, BLK], F32, name="hi_l")
+        lo_l = keep.tile([P, PACK, BLK], F32, name="lo_l")
+        part = keep.tile([P, PACK, BLK], F32, name="part")
+        full = keep.tile([P, PACK, BLK], F32, name="full")
+        nc.vector.scalar_tensor_tensor(hi_l[:], e1[:], 0.0, e2[:], ALU.max, ALU.max)
+        nc.vector.scalar_tensor_tensor(lo_l[:], e1[:], 0.0, e2[:], ALU.min, ALU.min)
+        for b in range(PE_BLKS):
+            quantize_and_score(b)
+        nc.scalar.activation(wide_a[0][:, 0:PE_COLS], scores[0][:, 0:PE_COLS], ACT.Copy, scale=0.0625)
+        for t in range(PACK):
+            nc.vector.scalar_tensor_tensor(
+                part[:, t, :], hi_l[:, t, :], alpha[:, t : t + 1], y_b[t][:, PE_COLS:S], ALU.mult, ALU.add
+            )
+        for t in range(PACK):
+            nc.vector.scalar_tensor_tensor(
+                full[:, t, :], lo_l[:, t, :], beta[:, t : t + 1], part[:, t, :], ALU.mult, ALU.add
+            )
+        nc.vector.tensor_scalar(
+            z_bf[PE_BLKS][:].rearrange("p (c i t) -> p c t i", i=4, t=PACK),
+            full[:].rearrange("p t (c i) -> p c t i", i=4),
+            0.5,
+            None,
+            ALU.mult,
+        )
+        quantize_and_score(PE_BLKS)
+        nc.scalar.activation(wide_a[0][:, PE_COLS:S], scores[0][:, PE_COLS:S], ACT.Copy, scale=0.0625)
+        for t in range(1, PACK):
+            nc.scalar.activation(wide_a[t][:, 0:S], scores[t][:], ACT.Copy, scale=0.0625)
+
+        out_rows = out.rearrange("(p t) j -> p t j", t=PACK)
+        g3, g4 = {}, {}
+
+        def fetch3(t):
+            g3[t] = ring.tile([P, S], F32, name="g3")
+            nc.vector.tensor_copy(g3[t][:], wide_a[t][:].indirect(n3_l[:]))
+
+        def larger(t):
+            nc.vector.tensor_tensor(wide_st[t][:, 0:S], wide_a[t][:, 0:S], g3[t][:], ALU.max)
+
+        def fetch4(t, lo_c, hi_c):
+            g4[t, lo_c] = ring.tile([P, hi_c - lo_c], F32, name="g4")
+            nc.vector.tensor_copy(g4[t, lo_c][:], wide_st[t][:].indirect(n4_l[:, lo_c // PER_COL : hi_c // PER_COL]))
+
+        def smaller(t, lo_c, hi_c):
+            res = keep.tile([P, hi_c - lo_c], F32, name=f"res{t}_{lo_c}")
+            nc.vector.tensor_tensor(res[:], wide_st[t][:, lo_c:hi_c], g4[t, lo_c][:], ALU.min)
+            nc.sync.dma_start(out_rows[:, t, lo_c:hi_c], res[:])
+
+        fetch3(0)
+        fetch3(1)
+        larger(0)
+        fetch3(2)
+        larger(1)
+        fetch4(0, 0, S)
+        larger(2)
+        fetch4(1, 0, S)
+        smaller(0, 0, S)
+        fetch3(3)
+        smaller(1, 0, S)
+        fetch4(2, 0, S)
+        larger(3)
+        smaller(2, 0, S)
+        fetch4(3, 0, S // 2)
+        fetch4(3, S // 2, S)
+        smaller(3, 0, S // 2)
+        smaller(3, S // 2, S)

@@ -24,7 +24,7 @@ PE_BLKS = NBLK - 1
 PE_COLS = PE_BLKS * BLK
 WIDE = 2 * S
 PER_COL = 16
-W_VEC = 44
+W_CHUNKS = ((0, 256), (256, 512))
 
 
 def tile_picked_hcandrangehopmn_none_p_kernel(
@@ -45,22 +45,33 @@ def tile_picked_hcandrangehopmn_none_p_kernel(
         table_bytes = keep.tile([P, T], U8, name="table_bytes", align_bytes=64)
         table_words = keep.tile([P, T], I32, name="table_words", align_bytes=64)
         gs_t = keep.tile([P, PACK], F32, name="gs_t")
-        w_raw = [keep.tile([P, PACK, H // 2], F32, name=f"w_raw{h}", align_bytes=64) for h in range(2)]
+        w_raw = [keep.tile([P, PACK, hi_c - lo_c], F32, name=f"w_raw{lo_c}") for lo_c, hi_c in W_CHUNKS]
 
+        w_rows = w1.rearrange("(p j) c -> p j c", j=PACK)
         nc.sync.dma_start(
             table_bytes[:].bitcast(I32), x_scales[0].bitcast(I32).unsqueeze(1).to_broadcast([16, 8, T // 4])
         )
         nc.sync.dma_start(offs_l[:], offs)
-        nc.sync.dma_start(gs_t[:], gs.rearrange("(p t) o -> p (t o)", t=PACK))
+        nc.sync.dma_start(w_raw[0][:], w_rows[:, :, 0 : H // 2])
         nc.sync.dma_start(cand_l[:], cand)
-        nc.sync.dma_start(table_words[:], x_words[0].rearrange("p c r -> p (c r)").bitcast(I32))
+        nc.sync.dma_start(gs_t[:], gs.rearrange("(p t) o -> p (t o)", t=PACK))
         nc.sync.dma_start(n1_l[:], n1)
         nc.sync.dma_start(n2_l[:], n2)
-        w_rows = w1.rearrange("(p j) c -> p j c", j=PACK)
-        for h in range(2):
-            nc.sync.dma_start(w_raw[h][:], w_rows[:, :, h * (H // 2) : (h + 1) * (H // 2)])
+        nc.sync.dma_start(w_raw[1][:], w_rows[:, :, H // 2 : H])
+        nc.sync.dma_start(table_words[:], x_words[0].rearrange("p c r -> p (c r)").bitcast(I32))
         nc.sync.dma_start(n3_l[:], n3)
         nc.sync.dma_start(n4_l[:], n4)
+
+        x_plane = keep.tile([P, S], U8, name="x_plane", align_bytes=64)
+        c_plane = keep.tile([P, C], U8, name="c_plane", align_bytes=64)
+        ident = keep.tile([P, P], F32, name="ident")
+        wide_a = [keep.tile([P, WIDE], F32, name=f"wide_a{t}") for t in range(PACK + 1)]
+        nc.gpsimd.memset(wide_a[PACK][:, S:], 0.0)
+        nc.gpsimd.memset(x_plane[:].bitcast(I32), 0)
+        nc.gpsimd.memset(c_plane[:].bitcast(I32), 0)
+        make_identity(nc, ident[:])
+        for t in range(PACK):
+            nc.scalar.activation(wide_a[t][:, S:], wide_a[PACK][:, S:], ACT.Copy)
 
         sign = keep.tile([P, PACK], F32, name="sign")
         alpha = keep.tile([P, PACK], F32, name="alpha")
@@ -69,54 +80,43 @@ def tile_picked_hcandrangehopmn_none_p_kernel(
         nc.scalar.activation(alpha[:], sign[:], ACT.Copy, scale=1.5, bias=0.5)
         nc.scalar.activation(beta[:], sign[:], ACT.Copy, scale=-1.5, bias=0.5)
 
-        x_plane = keep.tile([P, S], U8, name="x_plane", align_bytes=64)
-        c_plane = keep.tile([P, C], U8, name="c_plane", align_bytes=64)
-        ident = keep.tile([P, P], F32, name="ident")
-        wide_a = [keep.tile([P, WIDE], F32, name=f"wide_a{t}") for t in range(PACK)]
-        wide_st = [keep.tile([P, WIDE], F32, name=f"wide_st{t}") for t in range(PACK)]
-        nc.gpsimd.memset(x_plane[:].bitcast(I32), 0)
-        nc.gpsimd.memset(c_plane[:].bitcast(I32), 0)
-        for t in range(PACK):
-            nc.vector.memset(wide_a[t][:, S:], 0.0)
-        make_identity(nc, ident[:])
-        for t in range(PACK):
-            nc.gpsimd.memset(wide_st[t][:, S:], 0.0)
-
         def place_scale_rows(queue, plane, picked):
             for b in range(4):
                 queue.dma_start(plane[b:P:32, :].bitcast(I32), picked[8 * b : P : 32, :].bitcast(I32))
 
         x_bytes = keep.tile([P, S], U8, name="x_bytes", align_bytes=64)
         nc.vector.tensor_copy(x_bytes[:], table_bytes[:].indirect(offs_l[:]))
-        place_scale_rows(nc.scalar, x_plane, x_bytes)
+        place_scale_rows(nc.sync, x_plane, x_bytes)
 
         c_bytes = keep.tile([P, C], U8, name="c_bytes", align_bytes=64)
         nc.vector.tensor_copy(c_bytes[:], table_bytes[:].indirect(cand_l[:]))
 
-        x_codes = keep.tile([P, S], U32, name="x_codes", align_bytes=64)
-        nc.vector.tensor_copy(x_codes[:], table_words[:].bitcast(U32).indirect(offs_l[:]))
-
-        c_words = keep.tile([P, C], U32, name="c_words", align_bytes=64)
-        nc.vector.tensor_copy(c_words[:], table_words[:].bitcast(U32).indirect(cand_l[:]))
+        c_bytes_dealt = keep.tile([P, C], U8, name="c_bytes_dealt", align_bytes=64)
+        nc.vector.tensor_copy(
+            c_bytes_dealt[:].rearrange("p (t m) -> p m t", t=PACK), c_bytes[:].rearrange("p (m t) -> p m t", t=PACK)
+        )
+        place_scale_rows(nc.sync, c_plane, c_bytes_dealt)
 
         w_bf = keep.tile([P, PACK * H], BF16, name="w_bf", align_bytes=64)
         w_codes = keep.tile([P, H], U32, name="w_codes", align_bytes=64)
         w_plane = keep.tile([P, H], U8, name="w_plane", align_bytes=64)
         w_dst = w_bf[:].rearrange("p (t m j) -> p m j t", t=PACK, j=PACK)
         half = P // 2
-        nc.scalar.activation(w_dst[:, 0:half], w_raw[0][:].rearrange("p j (m t) -> p m j t", t=PACK), ACT.Copy)
-        w_late = w_raw[1][:].rearrange("p j (m t) -> p m j t", t=PACK)
-        nc.vector.tensor_copy(w_dst[:, half : half + W_VEC], w_late[:, 0:W_VEC])
-        nc.scalar.activation(w_dst[:, half + W_VEC : P], w_late[:, W_VEC:half], ACT.Copy)
+        for h in range(2):
+            nc.scalar.activation(
+                w_dst[:, h * half : (h + 1) * half], w_raw[h][:].rearrange("p j (m t) -> p m j t", t=PACK), ACT.Copy
+            )
+        nc.vector.quantize_mx(out=w_codes[:].bitcast(FP8X4), scales=w_plane[:], in_=w_bf[:])
+
+        x_codes = keep.tile([P, S], U32, name="x_codes", align_bytes=64)
+        for lo_c, hi_c in ((0, S // 2), (S // 2, S)):
+            nc.vector.tensor_copy(
+                x_codes[:, lo_c:hi_c], table_words[:].bitcast(U32).indirect(offs_l[:, lo_c // PER_COL : hi_c // PER_COL])
+            )
 
         y_b = [keep.tile([P, S], F32, name=f"y_b{t}") for t in range(PACK)]
         for t in range(PACK):
             cols = slice(t * P, (t + 1) * P)
-            nc.vector.quantize_mx(
-                out=w_codes[:, cols].bitcast(FP8X4),
-                scales=w_plane[:, cols],
-                in_=w_bf[:, t * PACK * P : (t + 1) * PACK * P],
-            )
             parts = [(0, S // 2, "acc0"), (S // 2, S, "acc_spare")] if t == 0 else [(0, S, f"acc{t}")]
             for lo_c, hi_c, bank in parts:
                 acc = psum.tile([P, hi_c - lo_c], F32, name=bank)
@@ -130,17 +130,11 @@ def tile_picked_hcandrangehopmn_none_p_kernel(
                     stop=True,
                 )
                 for dst in (wide_a[t], y_b[t]):
-                    if lo_c == 0:
-                        nc.scalar.activation(dst[:, lo_c:hi_c], acc[:], ACT.Copy, scale=gs_t[:, t : t + 1])
-                    else:
-                        nc.vector.tensor_scalar(dst[:, lo_c:hi_c], acc[:], gs_t[:, t : t + 1], None, ALU.mult)
+                    nc.scalar.activation(dst[:, lo_c:hi_c], acc[:], ACT.Copy, scale=gs_t[:, t : t + 1])
 
-        c_bytes_dealt = keep.tile([P, C], U8, name="w_raw1", align_bytes=64)
-        nc.vector.tensor_copy(
-            c_bytes_dealt[:].rearrange("p (t m) -> p m t", t=PACK), c_bytes[:].rearrange("p (m t) -> p m t", t=PACK)
-        )
-        place_scale_rows(nc.sync, c_plane, c_bytes_dealt)
-        c_codes = keep.tile([P, C], U32, name="w_bf", align_bytes=64)
+        c_words = keep.tile([P, C], U32, name="c_words", align_bytes=64)
+        nc.vector.tensor_copy(c_words[:], table_words[:].bitcast(U32).indirect(cand_l[:]))
+        c_codes = keep.tile([P, C], U32, name="c_codes", align_bytes=64)
         nc.vector.tensor_copy(
             c_codes[:].rearrange("p (t m) -> p m t", t=PACK), c_words[:].rearrange("p (m t) -> p m t", t=PACK)
         )
@@ -171,9 +165,9 @@ def tile_picked_hcandrangehopmn_none_p_kernel(
             lo_w = ring.tile([P, PE_COLS], F32, name="lo_w")
             nc.scalar.activation(hi_w[:], hi[:], ACT.Copy, scale=alpha[:, t : t + 1])
             nc.scalar.activation(lo_w[:], lo[:], ACT.Copy, scale=beta[:, t : t + 1])
-            for b in range(PE_BLKS):
-                cols = slice(b * BLK, (b + 1) * BLK)
-                for i, term in enumerate((y_b[t], hi_w, lo_w)):
+            for i, term in enumerate((y_b[t], hi_w, lo_w)):
+                for b in range(PE_BLKS):
+                    cols = slice(b * BLK, (b + 1) * BLK)
                     nc.tensor.matmul(
                         sums[b][:, t, :], lhsT=term[:, cols], rhs=ident[:], is_transpose=True, start=(i == 0), stop=(i == 2)
                     )
@@ -190,11 +184,11 @@ def tile_picked_hcandrangehopmn_none_p_kernel(
             if t + 1 < PACK:
                 first(t + 1)
             else:
-                e1 = keep.tile([P, PACK, BLK], F32, name="e1")
+                e1 = ring.tile([P, PACK, BLK], F32, name="d1")
                 nc.vector.tensor_tensor(e1[:, 0, :], y_b[0][:].indirect(n1_l[:, last]), wide_a[0][:, PE_COLS:S], ALU.subtract)
             combine(t)
 
-        z_bf = [keep.tile([P, BLK * PACK], BF16, name=f"z_bf{b}", align_bytes=64) for b in range(NBLK)]
+        z_bf = [keep.tile([P, BLK * PACK], BF16, name=f"z_bf{b}", align_bytes=64) for b in range(PE_BLKS)]
         z_codes = [keep.tile([P, BLK], U32, name=f"z_codes{b}", align_bytes=64) for b in range(NBLK)]
         z_plane = [keep.tile([P, BLK], U8, name=f"z_plane{b}", align_bytes=64) for b in range(NBLK)]
         for b in range(PE_BLKS):
@@ -208,7 +202,7 @@ def tile_picked_hcandrangehopmn_none_p_kernel(
 
         def quantize_and_score(b):
             nc.vector.quantize_mx(out=z_codes[b][:].bitcast(FP8X4), scales=z_plane[b][:], in_=z_bf[b][:])
-            for t in range(PACK):
+            for t in (0, 2, 3, 1):
                 cols = slice(t * P, (t + 1) * P)
                 nc.tensor.matmul_mx(
                     out=scores[t][:, b * BLK : (b + 1) * BLK],
@@ -220,28 +214,29 @@ def tile_picked_hcandrangehopmn_none_p_kernel(
                     stop=True,
                 )
 
-        e2 = keep.tile([P, PACK, BLK], F32, name="e2")
+        e2 = ring.tile([P, PACK, BLK], F32, name="d2")
         for t in range(PACK):
             if t > 0:
                 nc.vector.tensor_tensor(e1[:, t, :], y_b[t][:].indirect(n1_l[:, last]), wide_a[t][:, PE_COLS:S], ALU.subtract)
             nc.vector.tensor_tensor(e2[:, t, :], y_b[t][:].indirect(n2_l[:, last]), wide_a[t][:, PE_COLS:S], ALU.subtract)
         hi_l = keep.tile([P, PACK, BLK], F32, name="hi_l")
         lo_l = keep.tile([P, PACK, BLK], F32, name="lo_l")
-        part = keep.tile([P, PACK, BLK], F32, name="part")
-        full = keep.tile([P, PACK, BLK], F32, name="full")
         nc.vector.scalar_tensor_tensor(hi_l[:], e1[:], 0.0, e2[:], ALU.max, ALU.max)
         nc.vector.scalar_tensor_tensor(lo_l[:], e1[:], 0.0, e2[:], ALU.min, ALU.min)
-        for b in range(PE_BLKS):
-            quantize_and_score(b)
-        nc.scalar.activation(wide_a[0][:, 0:PE_COLS], scores[0][:, 0:PE_COLS], ACT.Copy, scale=0.0625)
+        part = keep.tile([P, PACK, BLK], F32, name="part")
         for t in range(PACK):
             nc.vector.scalar_tensor_tensor(
                 part[:, t, :], hi_l[:, t, :], alpha[:, t : t + 1], y_b[t][:, PE_COLS:S], ALU.mult, ALU.add
             )
+        quantize_and_score(0)
+        quantize_and_score(1)
+        full = keep.tile([P, PACK, BLK], F32, name="z_bf1", align_bytes=64)
         for t in range(PACK):
             nc.vector.scalar_tensor_tensor(
                 full[:, t, :], lo_l[:, t, :], beta[:, t : t + 1], part[:, t, :], ALU.mult, ALU.add
             )
+        quantize_and_score(2)
+        z_bf.append(keep.tile([P, BLK * PACK], BF16, name="z_bf2", align_bytes=64))
         nc.vector.tensor_scalar(
             z_bf[PE_BLKS][:].rearrange("p (c i t) -> p c t i", i=4, t=PACK),
             full[:].rearrange("p t (c i) -> p c t i", i=4),
@@ -249,23 +244,50 @@ def tile_picked_hcandrangehopmn_none_p_kernel(
             None,
             ALU.mult,
         )
-        quantize_and_score(PE_BLKS)
-        nc.scalar.activation(wide_a[0][:, PE_COLS:S], scores[0][:, PE_COLS:S], ACT.Copy, scale=0.0625)
-        for t in range(1, PACK):
-            nc.scalar.activation(wide_a[t][:, 0:S], scores[t][:], ACT.Copy, scale=0.0625)
 
         out_rows = out.rearrange("(p t) j -> p t j", t=PACK)
+        plain = {t: keep.tile([P, S], F32, name=f"plain{t}") for t in (2, 3)}
+        wide_st = [wide_a[2], wide_a[PACK], wide_a[0], wide_a[3]]
         g3, g4 = {}, {}
 
-        def fetch3(t):
-            g3[t] = ring.tile([P, S], F32, name="g3")
-            nc.vector.tensor_copy(g3[t][:], wide_a[t][:].indirect(n3_l[:]))
+        def score_out(t, lo_c, hi_c):
+            nc.scalar.activation(wide_a[t][:, lo_c:hi_c], scores[t][:, lo_c:hi_c], ACT.Copy, scale=0.0625)
+            if t in plain:
+                nc.scalar.activation(plain[t][:, lo_c:hi_c], scores[t][:, lo_c:hi_c], ACT.Copy, scale=0.0625)
 
-        def larger(t):
-            nc.vector.tensor_tensor(wide_st[t][:, 0:S], wide_a[t][:, 0:S], g3[t][:], ALU.max)
+        def diff3(t):
+            g3[t] = keep.tile([P, S], F32, name=f"d3_{t}")
+            nc.vector.tensor_tensor(g3[t][:], wide_a[t][:].indirect(n3_l[:]), plain[t][:], ALU.subtract)
+
+        turned = {}
+
+        def rise_and_turn(t):
+            rise = ring.tile([P, S], F32, name="rise")
+            nc.scalar.activation(rise[:], g3[t][:], ACT.Relu)
+            turned[t] = psum.tile([P, NBLK, P], F32, name=f"turn{t - 2}")
+            for i, term in enumerate((plain[t], rise)):
+                for k in range(NBLK):
+                    nc.tensor.matmul(
+                        turned[t][:, k, :],
+                        lhsT=term[:, k * BLK : (k + 1) * BLK],
+                        rhs=ident[:],
+                        is_transpose=True,
+                        start=(i == 0 and k == 0),
+                        stop=(i == 1 and k == NBLK - 1),
+                    )
+
+        def middle(t):
+            mid = ring.tile([P, NBLK, P], F32, name="mid")
+            nc.scalar.copy(mid[:], turned[t][:])
+            turned[t] = psum.tile([P, NBLK, BLK], F32, name=f"turn{t - 2}")
+            for k in range(NBLK):
+                nc.tensor.transpose(turned[t][:, k, :], mid[:, k, :], ident[:])
+
+        def land(t):
+            nc.scalar.copy(wide_st[t][:, 0:S], turned[t][:].rearrange("p k j -> p (k j)"))
 
         def fetch4(t, lo_c, hi_c):
-            g4[t, lo_c] = ring.tile([P, hi_c - lo_c], F32, name="g4")
+            g4[t, lo_c] = keep.tile([P, hi_c - lo_c], F32, name=f"g4_{t}_{lo_c}")
             nc.vector.tensor_copy(g4[t, lo_c][:], wide_st[t][:].indirect(n4_l[:, lo_c // PER_COL : hi_c // PER_COL]))
 
         def smaller(t, lo_c, hi_c):
@@ -273,21 +295,37 @@ def tile_picked_hcandrangehopmn_none_p_kernel(
             nc.vector.tensor_tensor(res[:], wide_st[t][:, lo_c:hi_c], g4[t, lo_c][:], ALU.min)
             nc.sync.dma_start(out_rows[:, t, lo_c:hi_c], res[:])
 
+        def fetch3(t):
+            g3[t] = keep.tile([P, S], F32, name=f"d3_{t}")
+            nc.vector.tensor_copy(g3[t][:], wide_a[t][:].indirect(n3_l[:]))
+
+        def larger(t):
+            nc.vector.tensor_tensor(wide_st[t][:, 0:S], wide_a[t][:, 0:S], g3[t][:], ALU.max)
+
+        score_out(0, 0, PE_COLS)
+        quantize_and_score(PE_BLKS)
+        score_out(0, PE_COLS, S)
+        for t in (2, 3, 1):
+            score_out(t, 0, S)
         fetch3(0)
-        fetch3(1)
+        diff3(2)
         larger(0)
-        fetch3(2)
-        larger(1)
+        diff3(3)
+        rise_and_turn(2)
+        rise_and_turn(3)
+        middle(2)
+        middle(3)
+        land(2)
+        land(3)
+        fetch3(1)
         fetch4(0, 0, S)
-        larger(2)
-        fetch4(1, 0, S)
+        larger(1)
         smaller(0, 0, S)
-        fetch3(3)
-        smaller(1, 0, S)
+        fetch4(1, 0, S)
         fetch4(2, 0, S)
-        larger(3)
-        smaller(2, 0, S)
+        smaller(1, 0, S)
         fetch4(3, 0, S // 2)
+        smaller(2, 0, S)
         fetch4(3, S // 2, S)
         smaller(3, 0, S // 2)
         smaller(3, S // 2, S)

@@ -70,15 +70,7 @@ def tile_picked_hcandrangehopmn_none_p_kernel(
         nc.gpsimd.memset(x_plane[:].bitcast(I32), 0)
         nc.gpsimd.memset(c_plane[:].bitcast(I32), 0)
         make_identity(nc, ident[:])
-        for t in range(PACK):
-            nc.scalar.activation(wide_a[t][:, S:], wide_a[PACK][:, S:], ACT.Copy)
-
-        sign = keep.tile([P, PACK], F32, name="sign")
-        alpha = keep.tile([P, PACK], F32, name="alpha")
-        beta = keep.tile([P, PACK], F32, name="beta")
-        nc.scalar.activation(sign[:], gs_t[:], ACT.Sign)
-        nc.scalar.activation(alpha[:], sign[:], ACT.Copy, scale=1.5, bias=0.5)
-        nc.scalar.activation(beta[:], sign[:], ACT.Copy, scale=-1.5, bias=0.5)
+        nc.scalar.activation(wide_a[0][:, S:], wide_a[PACK][:, S:], ACT.Copy)
 
         def place_scale_rows(queue, plane, picked):
             for b in range(4):
@@ -102,13 +94,21 @@ def tile_picked_hcandrangehopmn_none_p_kernel(
         w_plane = keep.tile([P, H], U8, name="w_plane", align_bytes=64)
         w_dst = w_bf[:].rearrange("p (t m j) -> p m j t", t=PACK, j=PACK)
         half = P // 2
-        for h in range(2):
-            nc.scalar.activation(
-                w_dst[:, h * half : (h + 1) * half], w_raw[h][:].rearrange("p j (m t) -> p m j t", t=PACK), ACT.Copy
-            )
+        nc.scalar.activation(w_dst[:, 0:half], w_raw[0][:].rearrange("p j (m t) -> p m j t", t=PACK), ACT.Copy)
+        nc.vector.tensor_copy(w_dst[:, half:P], w_raw[1][:].rearrange("p j (m t) -> p m j t", t=PACK))
         nc.vector.quantize_mx(out=w_codes[:].bitcast(FP8X4), scales=w_plane[:], in_=w_bf[:])
 
-        x_codes = keep.tile([P, S], U32, name="x_codes", align_bytes=64)
+        sign = keep.tile([P, PACK], F32, name="sign")
+        alpha = keep.tile([P, PACK], F32, name="alpha")
+        beta = keep.tile([P, PACK], F32, name="beta")
+        nc.scalar.activation(sign[:], gs_t[:], ACT.Sign)
+        nc.scalar.activation(alpha[:], sign[:], ACT.Copy, scale=1.5, bias=0.5)
+        nc.scalar.activation(beta[:], sign[:], ACT.Copy, scale=-1.5, bias=0.5)
+
+        for t in range(1, PACK):
+            nc.scalar.activation(wide_a[t][:, S:], wide_a[PACK][:, S:], ACT.Copy)
+
+        x_codes = keep.tile([P, S], U32, name="w_bf", align_bytes=64)
         for lo_c, hi_c in ((0, S // 2), (S // 2, S)):
             nc.vector.tensor_copy(
                 x_codes[:, lo_c:hi_c], table_words[:].bitcast(U32).indirect(offs_l[:, lo_c // PER_COL : hi_c // PER_COL])
@@ -261,14 +261,14 @@ def tile_picked_hcandrangehopmn_none_p_kernel(
 
         turned = {}
 
-        def rise_and_turn(t):
-            rise = ring.tile([P, S], F32, name="rise")
-            nc.scalar.activation(rise[:], g3[t][:], ACT.Relu)
-            turned[t] = psum.tile([P, NBLK, P], F32, name=f"turn{t - 2}")
-            for i, term in enumerate((plain[t], rise)):
+        def turn(bank, base, gap, sense):
+            step = ring.tile([P, S], F32, name="step")
+            nc.scalar.activation(step[:], gap[:], ACT.Relu, scale=sense)
+            turned[bank] = psum.tile([P, NBLK, P], F32, name=f"turn{bank}")
+            for i, term in enumerate((base, step)):
                 for k in range(NBLK):
                     nc.tensor.matmul(
-                        turned[t][:, k, :],
+                        turned[bank][:, k, :],
                         lhsT=term[:, k * BLK : (k + 1) * BLK],
                         rhs=ident[:],
                         is_transpose=True,
@@ -276,15 +276,15 @@ def tile_picked_hcandrangehopmn_none_p_kernel(
                         stop=(i == 1 and k == NBLK - 1),
                     )
 
-        def middle(t):
+        def middle(bank):
             mid = ring.tile([P, NBLK, P], F32, name="mid")
-            nc.scalar.copy(mid[:], turned[t][:])
-            turned[t] = psum.tile([P, NBLK, BLK], F32, name=f"turn{t - 2}")
+            nc.scalar.copy(mid[:], turned[bank][:])
+            turned[bank] = psum.tile([P, NBLK, BLK], F32, name=f"turn{bank}")
             for k in range(NBLK):
-                nc.tensor.transpose(turned[t][:, k, :], mid[:, k, :], ident[:])
+                nc.tensor.transpose(turned[bank][:, k, :], mid[:, k, :], ident[:])
 
-        def land(t):
-            nc.scalar.copy(wide_st[t][:, 0:S], turned[t][:].rearrange("p k j -> p (k j)"))
+        def land(bank, dst, sense):
+            nc.scalar.activation(dst, turned[bank][:].rearrange("p k j -> p (k j)"), ACT.Copy, scale=sense)
 
         def fetch4(t, lo_c, hi_c):
             g4[t, lo_c] = keep.tile([P, hi_c - lo_c], F32, name=f"g4_{t}_{lo_c}")
@@ -311,16 +311,23 @@ def tile_picked_hcandrangehopmn_none_p_kernel(
         diff3(2)
         larger(0)
         diff3(3)
-        rise_and_turn(2)
-        rise_and_turn(3)
-        middle(2)
-        middle(3)
-        land(2)
-        land(3)
+        turn(0, plain[2], g3[2], 1.0)
+        neg = keep.tile([P, S], F32, name="neg")
+        nc.scalar.activation(neg[:], wide_st[0][:, 0:S], ACT.Copy, scale=-1.0)
+        middle(0)
+        turn(1, plain[3], g3[3], 1.0)
+        land(0, wide_st[2][:, 0:S], 1.0)
+        middle(1)
+        land(1, wide_st[3][:, 0:S], 1.0)
         fetch3(1)
-        fetch4(0, 0, S)
+        gap4 = keep.tile([P, S], F32, name="gap4")
+        nc.vector.tensor_tensor(gap4[:], wide_st[0][:].indirect(n4_l[:]), neg[:], ALU.add)
         larger(1)
-        smaller(0, 0, S)
+        turn(2, neg, gap4, -1.0)
+        middle(2)
+        res0 = keep.tile([P, S], F32, name="res0")
+        land(2, res0[:], -1.0)
+        nc.sync.dma_start(out_rows[:, 0, :], res0[:])
         fetch4(1, 0, S)
         fetch4(2, 0, S)
         smaller(1, 0, S)

@@ -18,13 +18,18 @@ ACT = mybir.ActivationFunctionType
 
 P = 128
 PACK = 4
+SCALE_ROWS = K // 32
+BLOCK_PARTS = P // SCALE_ROWS
+QUADRANT = 32
+PER_COL = 16
 BLK = 128
 NBLK = S // BLK
 PE_BLKS = NBLK - 1
 PE_COLS = PE_BLKS * BLK
 WIDE = 2 * S
-PER_COL = 16
-W_CHUNKS = ((0, 256), (256, 512))
+SCORE_SCALE = 0.0625
+PE_MAX_TILES = (2, 3)
+SCORE_ORDER = (0, 2, 3, 1)
 
 
 def tile_picked_hcandrangehopmn_none_p_kernel(
@@ -39,300 +44,315 @@ def tile_picked_hcandrangehopmn_none_p_kernel(
         def list_tile(name):
             return keep.tile([P, S // PER_COL], U16, name=name)
 
+        def entries(lst, lo_c, hi_c):
+            return lst[:, lo_c // PER_COL : hi_c // PER_COL]
+
         offs_l, cand_l = list_tile("offs_l"), list_tile("cand_l")
         n1_l, n2_l, n3_l, n4_l = (list_tile(n) for n in ("n1_l", "n2_l", "n3_l", "n4_l"))
+        halves = ((0, S // 2), (S // 2, S))
 
         table_bytes = keep.tile([P, T], U8, name="table_bytes", align_bytes=64)
         table_words = keep.tile([P, T], I32, name="table_words", align_bytes=64)
         gs_t = keep.tile([P, PACK], F32, name="gs_t")
-        w_raw = [keep.tile([P, PACK, hi_c - lo_c], F32, name=f"w_raw{lo_c}") for lo_c, hi_c in W_CHUNKS]
+        w_raw = [keep.tile([P, PACK, H // 2], F32, name=f"w_raw{h}") for h in range(2)]
 
         w_rows = w1.rearrange("(p j) c -> p j c", j=PACK)
         nc.sync.dma_start(
-            table_bytes[:].bitcast(I32), x_scales[0].bitcast(I32).unsqueeze(1).to_broadcast([16, 8, T // 4])
+            table_bytes[:].bitcast(I32),
+            x_scales[0].bitcast(I32).unsqueeze(1).to_broadcast([SCALE_ROWS, BLOCK_PARTS, T // 4]),
         )
         nc.sync.dma_start(offs_l[:], offs)
-        nc.sync.dma_start(w_raw[0][:], w_rows[:, :, 0 : H // 2])
         nc.sync.dma_start(cand_l[:], cand)
-        nc.sync.dma_start(gs_t[:], gs.rearrange("(p t) o -> p (t o)", t=PACK))
-        nc.sync.dma_start(n1_l[:], n1)
-        nc.sync.dma_start(n2_l[:], n2)
+        nc.sync.dma_start(w_raw[0][:], w_rows[:, :, 0 : H // 2])
         nc.sync.dma_start(w_raw[1][:], w_rows[:, :, H // 2 : H])
         nc.sync.dma_start(table_words[:], x_words[0].rearrange("p c r -> p (c r)").bitcast(I32))
-        nc.sync.dma_start(n3_l[:], n3)
-        nc.sync.dma_start(n4_l[:], n4)
 
         x_plane = keep.tile([P, S], U8, name="x_plane", align_bytes=64)
         c_plane = keep.tile([P, C], U8, name="c_plane", align_bytes=64)
         ident = keep.tile([P, P], F32, name="ident")
-        wide_a = [keep.tile([P, WIDE], F32, name=f"wide_a{t}") for t in range(PACK + 1)]
-        nc.gpsimd.memset(wide_a[PACK][:, S:], 0.0)
+        wide = [keep.tile([P, WIDE], F32, name=f"wide{t}") for t in range(PACK + 1)]
+        nc.gpsimd.memset(wide[PACK][:, S:], 0.0)
         nc.gpsimd.memset(x_plane[:].bitcast(I32), 0)
         nc.gpsimd.memset(c_plane[:].bitcast(I32), 0)
         make_identity(nc, ident[:])
-        nc.scalar.activation(wide_a[0][:, S:], wide_a[PACK][:, S:], ACT.Copy)
+        nc.scalar.activation(wide[0][:, S:], wide[PACK][:, S:], ACT.Copy)
 
-        def place_scale_rows(queue, plane, picked):
-            for b in range(4):
-                queue.dma_start(plane[b:P:32, :].bitcast(I32), picked[8 * b : P : 32, :].bitcast(I32))
+        def place_scale_rows(plane, picked):
+            for b in range(QUADRANT // BLOCK_PARTS):
+                nc.sync.dma_start(
+                    plane[b:P:QUADRANT, :].bitcast(I32), picked[BLOCK_PARTS * b : P : QUADRANT, :].bitcast(I32)
+                )
+
+        def deal(dealt, picked):
+            nc.vector.tensor_copy(
+                dealt[:].rearrange("p (t m) -> p m t", t=PACK), picked[:].rearrange("p (m t) -> p m t", t=PACK)
+            )
 
         x_bytes = keep.tile([P, S], U8, name="x_bytes", align_bytes=64)
         nc.vector.tensor_copy(x_bytes[:], table_bytes[:].indirect(offs_l[:]))
-        place_scale_rows(nc.sync, x_plane, x_bytes)
+        place_scale_rows(x_plane, x_bytes)
+        nc.sync.dma_start(gs_t[:], gs.rearrange("(p t) o -> p (t o)", t=PACK))
+        nc.sync.dma_start(n1_l[:], n1)
+        nc.sync.dma_start(n2_l[:], n2)
+        nc.sync.dma_start(n3_l[:], n3)
+        nc.sync.dma_start(n4_l[:], n4)
 
         c_bytes = keep.tile([P, C], U8, name="c_bytes", align_bytes=64)
         nc.vector.tensor_copy(c_bytes[:], table_bytes[:].indirect(cand_l[:]))
-
         c_bytes_dealt = keep.tile([P, C], U8, name="c_bytes_dealt", align_bytes=64)
-        nc.vector.tensor_copy(
-            c_bytes_dealt[:].rearrange("p (t m) -> p m t", t=PACK), c_bytes[:].rearrange("p (m t) -> p m t", t=PACK)
-        )
-        place_scale_rows(nc.sync, c_plane, c_bytes_dealt)
+        deal(c_bytes_dealt, c_bytes)
+        place_scale_rows(c_plane, c_bytes_dealt)
 
-        w_bf = keep.tile([P, PACK * H], BF16, name="w_bf", align_bytes=64)
+        w_bf = keep.tile([P, PACK * H], BF16, name="w_bf", tag="w_bf", align_bytes=64)
         w_codes = keep.tile([P, H], U32, name="w_codes", align_bytes=64)
         w_plane = keep.tile([P, H], U8, name="w_plane", align_bytes=64)
         w_dst = w_bf[:].rearrange("p (t m j) -> p m j t", t=PACK, j=PACK)
-        half = P // 2
-        nc.scalar.activation(w_dst[:, 0:half], w_raw[0][:].rearrange("p j (m t) -> p m j t", t=PACK), ACT.Copy)
-        nc.vector.tensor_copy(w_dst[:, half:P], w_raw[1][:].rearrange("p j (m t) -> p m j t", t=PACK))
+        nc.scalar.activation(w_dst[:, 0 : P // 2], w_raw[0][:].rearrange("p j (m t) -> p m j t", t=PACK), ACT.Copy)
+        nc.vector.tensor_copy(w_dst[:, P // 2 : P], w_raw[1][:].rearrange("p j (m t) -> p m j t", t=PACK))
         nc.vector.quantize_mx(out=w_codes[:].bitcast(FP8X4), scales=w_plane[:], in_=w_bf[:])
 
-        sign = keep.tile([P, PACK], F32, name="sign")
-        alpha = keep.tile([P, PACK], F32, name="alpha")
-        beta = keep.tile([P, PACK], F32, name="beta")
-        nc.scalar.activation(sign[:], gs_t[:], ACT.Sign)
-        nc.scalar.activation(alpha[:], sign[:], ACT.Copy, scale=1.5, bias=0.5)
-        nc.scalar.activation(beta[:], sign[:], ACT.Copy, scale=-1.5, bias=0.5)
+        gs_sign = keep.tile([P, PACK], F32, name="gs_sign")
+        hi_weight = keep.tile([P, PACK], F32, name="hi_weight")
+        lo_weight = keep.tile([P, PACK], F32, name="lo_weight")
+        nc.scalar.activation(gs_sign[:], gs_t[:], ACT.Sign)
+        nc.scalar.activation(hi_weight[:], gs_sign[:], ACT.Copy, scale=1.5, bias=0.5)
+        nc.scalar.activation(lo_weight[:], gs_sign[:], ACT.Copy, scale=-1.5, bias=0.5)
 
         for t in range(1, PACK):
-            nc.scalar.activation(wide_a[t][:, S:], wide_a[PACK][:, S:], ACT.Copy)
+            nc.scalar.activation(wide[t][:, S:], wide[PACK][:, S:], ACT.Copy)
 
-        x_codes = keep.tile([P, S], U32, name="w_bf", align_bytes=64)
-        for lo_c, hi_c in ((0, S // 2), (S // 2, S)):
+        x_codes = keep.tile([P, S], U32, name="x_codes", tag="w_bf", align_bytes=64)
+        for lo_c, hi_c in halves:
             nc.vector.tensor_copy(
-                x_codes[:, lo_c:hi_c], table_words[:].bitcast(U32).indirect(offs_l[:, lo_c // PER_COL : hi_c // PER_COL])
+                x_codes[:, lo_c:hi_c], table_words[:].bitcast(U32).indirect(entries(offs_l, lo_c, hi_c))
             )
 
-        y_b = [keep.tile([P, S], F32, name=f"y_b{t}") for t in range(PACK)]
+        v_plain = [keep.tile([P, S], F32, name=f"v_plain{t}") for t in range(PACK)]
         for t in range(PACK):
-            cols = slice(t * P, (t + 1) * P)
-            parts = [(0, S // 2, "acc0"), (S // 2, S, "acc_spare")] if t == 0 else [(0, S, f"acc{t}")]
-            for lo_c, hi_c, bank in parts:
-                acc = psum.tile([P, hi_c - lo_c], F32, name=bank)
+            rows = slice(t * P, (t + 1) * P)
+            parts = zip(halves, ("acc0", "acc_half")) if t == 0 else [((0, S), f"acc{t}")]
+            for (lo_c, hi_c), bank in parts:
+                y_acc = psum.tile([P, hi_c - lo_c], F32, name="y_acc", tag=bank)
                 nc.tensor.matmul_mx(
-                    out=acc[:],
-                    lhsT=w_codes[:, cols].bitcast(FP8X4),
-                    lhsT_scale=w_plane[:, cols],
+                    out=y_acc[:],
+                    lhsT=w_codes[:, rows].bitcast(FP8X4),
+                    lhsT_scale=w_plane[:, rows],
                     rhs=x_codes[:, lo_c:hi_c].bitcast(FP8X4),
                     rhs_scale=x_plane[:, lo_c:hi_c],
                     start=True,
                     stop=True,
                 )
-                for dst in (wide_a[t], y_b[t]):
-                    nc.scalar.activation(dst[:, lo_c:hi_c], acc[:], ACT.Copy, scale=gs_t[:, t : t + 1])
+                for dst in (wide[t], v_plain[t]):
+                    nc.scalar.activation(dst[:, lo_c:hi_c], y_acc[:], ACT.Copy, scale=gs_t[:, t : t + 1])
 
         c_words = keep.tile([P, C], U32, name="c_words", align_bytes=64)
         nc.vector.tensor_copy(c_words[:], table_words[:].bitcast(U32).indirect(cand_l[:]))
         c_codes = keep.tile([P, C], U32, name="c_codes", align_bytes=64)
-        nc.vector.tensor_copy(
-            c_codes[:].rearrange("p (t m) -> p m t", t=PACK), c_words[:].rearrange("p (m t) -> p m t", t=PACK)
-        )
+        deal(c_codes, c_words)
 
-        lead = slice(0, PE_COLS // PER_COL)
-        last = slice(PE_COLS // PER_COL, S // PER_COL)
-        sums = [psum.tile([P, PACK, P], F32, name=f"turn{b}") for b in range(PE_BLKS)]
+        z_sums = [psum.tile([P, PACK, P], F32, name="z_sums", tag=f"turn{b}") for b in range(PE_BLKS)]
         z_turned = [keep.tile([P, 2, P, 2], BF16, name=f"z_turned{b}", align_bytes=64) for b in range(PE_BLKS)]
-        d1, d2 = {}, {}
 
-        def diff(dst, t, lst):
-            nc.vector.tensor_tensor(dst[:], wide_a[t][:].indirect(lst[:, lead]), y_b[t][:, 0:PE_COLS], ALU.subtract)
+        def lead_diff(t, lst, tag):
+            d = ring.tile([P, PE_COLS], F32, name="d", tag=tag)
+            nc.vector.tensor_tensor(
+                d[:], wide[t][:].indirect(entries(lst, 0, PE_COLS)), v_plain[t][:, 0:PE_COLS], ALU.subtract
+            )
+            return d
 
-        def first(t):
-            d1[t] = ring.tile([P, PE_COLS], F32, name="d1")
-            diff(d1[t], t, n1_l)
+        def last_diff(d, t, lst):
+            nc.vector.tensor_tensor(
+                d[:, t, :], v_plain[t][:].indirect(entries(lst, PE_COLS, S)), wide[t][:, PE_COLS:S], ALU.subtract
+            )
 
-        def second(t):
-            d2[t] = ring.tile([P, PE_COLS], F32, name="d2")
-            diff(d2[t], t, n2_l)
-
-        def combine(t):
+        def lead_sum(t, d1, d2):
             hi = ring.tile([P, PE_COLS], F32, name="hi")
             lo = ring.tile([P, PE_COLS], F32, name="lo")
-            nc.vector.scalar_tensor_tensor(hi[:], d1[t][:], 0.0, d2[t][:], ALU.max, ALU.max)
-            nc.vector.scalar_tensor_tensor(lo[:], d1[t][:], 0.0, d2[t][:], ALU.min, ALU.min)
-            hi_w = ring.tile([P, PE_COLS], F32, name="hi_w")
-            lo_w = ring.tile([P, PE_COLS], F32, name="lo_w")
-            nc.scalar.activation(hi_w[:], hi[:], ACT.Copy, scale=alpha[:, t : t + 1])
-            nc.scalar.activation(lo_w[:], lo[:], ACT.Copy, scale=beta[:, t : t + 1])
-            for i, term in enumerate((y_b[t], hi_w, lo_w)):
+            nc.vector.scalar_tensor_tensor(hi[:], d1[:], 0.0, d2[:], ALU.max, ALU.max)
+            nc.vector.scalar_tensor_tensor(lo[:], d1[:], 0.0, d2[:], ALU.min, ALU.min)
+            hi_term = ring.tile([P, PE_COLS], F32, name="hi_term")
+            lo_term = ring.tile([P, PE_COLS], F32, name="lo_term")
+            nc.scalar.activation(hi_term[:], hi[:], ACT.Copy, scale=hi_weight[:, t : t + 1])
+            nc.scalar.activation(lo_term[:], lo[:], ACT.Copy, scale=lo_weight[:, t : t + 1])
+            terms = (v_plain[t], hi_term, lo_term)
+            for i, term in enumerate(terms):
                 for b in range(PE_BLKS):
-                    cols = slice(b * BLK, (b + 1) * BLK)
                     nc.tensor.matmul(
-                        sums[b][:, t, :], lhsT=term[:, cols], rhs=ident[:], is_transpose=True, start=(i == 0), stop=(i == 2)
+                        z_sums[b][:, t, :],
+                        lhsT=term[:, b * BLK : (b + 1) * BLK],
+                        rhs=ident[:],
+                        is_transpose=True,
+                        start=(i == 0),
+                        stop=(i == len(terms) - 1),
                     )
             if t % 2 == 1:
                 u = t // 2
                 for b in range(PE_BLKS):
                     nc.scalar.activation(
-                        z_turned[b][:, u], sums[b][:, 2 * u : 2 * u + 2, :].rearrange("j e p -> j p e"), ACT.Copy, scale=0.5
+                        z_turned[b][:, u],
+                        z_sums[b][:, 2 * u : 2 * u + 2, :].rearrange("j e p -> j p e"),
+                        ACT.Copy,
+                        scale=0.5,
                     )
 
-        first(0)
+        d1_next = lead_diff(0, n1_l, "d1")
         for t in range(PACK):
-            second(t)
+            d1_now = d1_next
+            d2_now = lead_diff(t, n2_l, "d2")
             if t + 1 < PACK:
-                first(t + 1)
+                d1_next = lead_diff(t + 1, n1_l, "d1")
             else:
-                e1 = ring.tile([P, PACK, BLK], F32, name="d1")
-                nc.vector.tensor_tensor(e1[:, 0, :], y_b[0][:].indirect(n1_l[:, last]), wide_a[0][:, PE_COLS:S], ALU.subtract)
-            combine(t)
+                d1_last = ring.tile([P, PACK, BLK], F32, name="d1_last", tag="d1")
+                last_diff(d1_last, 0, n1_l)
+            lead_sum(t, d1_now, d2_now)
 
-        z_bf = [keep.tile([P, BLK * PACK], BF16, name=f"z_bf{b}", align_bytes=64) for b in range(PE_BLKS)]
+        z_bf = [keep.tile([P, BLK * PACK], BF16, name="z_bf", tag=f"z_bf{b}", align_bytes=64) for b in range(PE_BLKS)]
         z_codes = [keep.tile([P, BLK], U32, name=f"z_codes{b}", align_bytes=64) for b in range(NBLK)]
         z_plane = [keep.tile([P, BLK], U8, name=f"z_plane{b}", align_bytes=64) for b in range(NBLK)]
         for b in range(PE_BLKS):
-            back = psum.tile([P, 2, BLK], F32, name=f"turn{b}")
-            words = z_turned[b][:].rearrange("j u p e -> j (u p e)").bitcast(F32)
+            z_pairs = psum.tile([P, 2, BLK], F32, name="z_pairs", tag=f"turn{b}")
+            pair_words = z_turned[b][:].rearrange("j u p e -> j (u p e)").bitcast(F32)
             for u in range(2):
-                nc.tensor.transpose(back[:, u, :], words[:, u * P : (u + 1) * P], ident[:])
-            nc.scalar.copy(z_bf[b][:].bitcast(F32).rearrange("p (j u) -> p j u", u=2), back[:].rearrange("p u j -> p j u"))
+                nc.tensor.transpose(z_pairs[:, u, :], pair_words[:, u * P : (u + 1) * P], ident[:])
+            nc.scalar.copy(
+                z_bf[b][:].bitcast(F32).rearrange("p (j u) -> p j u", u=2), z_pairs[:].rearrange("p u j -> p j u")
+            )
 
-        scores = [psum.tile([P, S], F32, name=f"acc{t}") for t in range(PACK)]
+        s_acc = [psum.tile([P, S], F32, name="s_acc", tag=f"acc{t}") for t in range(PACK)]
 
         def quantize_and_score(b):
             nc.vector.quantize_mx(out=z_codes[b][:].bitcast(FP8X4), scales=z_plane[b][:], in_=z_bf[b][:])
-            for t in (0, 2, 3, 1):
-                cols = slice(t * P, (t + 1) * P)
+            for t in SCORE_ORDER:
+                rows = slice(t * P, (t + 1) * P)
                 nc.tensor.matmul_mx(
-                    out=scores[t][:, b * BLK : (b + 1) * BLK],
-                    lhsT=c_codes[:, cols].bitcast(FP8X4),
-                    lhsT_scale=c_plane[:, cols],
+                    out=s_acc[t][:, b * BLK : (b + 1) * BLK],
+                    lhsT=c_codes[:, rows].bitcast(FP8X4),
+                    lhsT_scale=c_plane[:, rows],
                     rhs=z_codes[b][:].bitcast(FP8X4),
                     rhs_scale=z_plane[b][:],
                     start=True,
                     stop=True,
                 )
 
-        e2 = ring.tile([P, PACK, BLK], F32, name="d2")
+        d2_last = ring.tile([P, PACK, BLK], F32, name="d2_last", tag="d2")
         for t in range(PACK):
             if t > 0:
-                nc.vector.tensor_tensor(e1[:, t, :], y_b[t][:].indirect(n1_l[:, last]), wide_a[t][:, PE_COLS:S], ALU.subtract)
-            nc.vector.tensor_tensor(e2[:, t, :], y_b[t][:].indirect(n2_l[:, last]), wide_a[t][:, PE_COLS:S], ALU.subtract)
-        hi_l = keep.tile([P, PACK, BLK], F32, name="hi_l")
-        lo_l = keep.tile([P, PACK, BLK], F32, name="lo_l")
-        nc.vector.scalar_tensor_tensor(hi_l[:], e1[:], 0.0, e2[:], ALU.max, ALU.max)
-        nc.vector.scalar_tensor_tensor(lo_l[:], e1[:], 0.0, e2[:], ALU.min, ALU.min)
-        part = keep.tile([P, PACK, BLK], F32, name="part")
+                last_diff(d1_last, t, n1_l)
+            last_diff(d2_last, t, n2_l)
+        hi_last = keep.tile([P, PACK, BLK], F32, name="hi_last")
+        lo_last = keep.tile([P, PACK, BLK], F32, name="lo_last")
+        nc.vector.scalar_tensor_tensor(hi_last[:], d1_last[:], 0.0, d2_last[:], ALU.max, ALU.max)
+        nc.vector.scalar_tensor_tensor(lo_last[:], d1_last[:], 0.0, d2_last[:], ALU.min, ALU.min)
+        z_part = keep.tile([P, PACK, BLK], F32, name="z_part")
         for t in range(PACK):
             nc.vector.scalar_tensor_tensor(
-                part[:, t, :], hi_l[:, t, :], alpha[:, t : t + 1], y_b[t][:, PE_COLS:S], ALU.mult, ALU.add
+                z_part[:, t, :], hi_last[:, t, :], hi_weight[:, t : t + 1], v_plain[t][:, PE_COLS:S], ALU.mult, ALU.add
             )
         quantize_and_score(0)
         quantize_and_score(1)
-        full = keep.tile([P, PACK, BLK], F32, name="z_bf1", align_bytes=64)
+        z_twice = keep.tile([P, PACK, BLK], F32, name="z_twice", tag="z_bf1", align_bytes=64)
         for t in range(PACK):
             nc.vector.scalar_tensor_tensor(
-                full[:, t, :], lo_l[:, t, :], beta[:, t : t + 1], part[:, t, :], ALU.mult, ALU.add
+                z_twice[:, t, :], lo_last[:, t, :], lo_weight[:, t : t + 1], z_part[:, t, :], ALU.mult, ALU.add
             )
         quantize_and_score(2)
-        z_bf.append(keep.tile([P, BLK * PACK], BF16, name="z_bf2", align_bytes=64))
+        z_bf.append(keep.tile([P, BLK * PACK], BF16, name="z_bf_last", tag="z_bf2", align_bytes=64))
         nc.vector.tensor_scalar(
             z_bf[PE_BLKS][:].rearrange("p (c i t) -> p c t i", i=4, t=PACK),
-            full[:].rearrange("p t (c i) -> p c t i", i=4),
+            z_twice[:].rearrange("p t (c i) -> p c t i", i=4),
             0.5,
             None,
             ALU.mult,
         )
 
         out_rows = out.rearrange("(p t) j -> p t j", t=PACK)
-        plain = {t: keep.tile([P, S], F32, name=f"plain{t}") for t in (2, 3)}
-        wide_st = [wide_a[2], wide_a[PACK], wide_a[0], wide_a[3]]
-        g3, g4 = {}, {}
+        s_plain = {t: keep.tile([P, S], F32, name=f"s_plain{t}") for t in PE_MAX_TILES}
+        st_wide = [wide[2], wide[PACK], wide[0], wide[3]]
+        by_n3, by_n4, in_bank = {}, {}, {}
 
         def score_out(t, lo_c, hi_c):
-            nc.scalar.activation(wide_a[t][:, lo_c:hi_c], scores[t][:, lo_c:hi_c], ACT.Copy, scale=0.0625)
-            if t in plain:
-                nc.scalar.activation(plain[t][:, lo_c:hi_c], scores[t][:, lo_c:hi_c], ACT.Copy, scale=0.0625)
+            nc.scalar.activation(wide[t][:, lo_c:hi_c], s_acc[t][:, lo_c:hi_c], ACT.Copy, scale=SCORE_SCALE)
+            if t in s_plain:
+                nc.scalar.activation(s_plain[t][:, lo_c:hi_c], s_acc[t][:, lo_c:hi_c], ACT.Copy, scale=SCORE_SCALE)
 
-        def diff3(t):
-            g3[t] = keep.tile([P, S], F32, name=f"d3_{t}")
-            nc.vector.tensor_tensor(g3[t][:], wide_a[t][:].indirect(n3_l[:]), plain[t][:], ALU.subtract)
+        def fetch_n3(t):
+            by_n3[t] = keep.tile([P, S], F32, name=f"by_n3_{t}")
+            nc.vector.tensor_copy(by_n3[t][:], wide[t][:].indirect(n3_l[:]))
 
-        turned = {}
+        def diff_n3(t):
+            by_n3[t] = keep.tile([P, S], F32, name=f"by_n3_{t}")
+            nc.vector.tensor_tensor(by_n3[t][:], wide[t][:].indirect(n3_l[:]), s_plain[t][:], ALU.subtract)
 
-        def turn(bank, base, gap, sense):
+        def larger(t):
+            nc.vector.tensor_tensor(st_wide[t][:, 0:S], wide[t][:, 0:S], by_n3[t][:], ALU.max)
+
+        def sum_turned(bank, base, gap, sense):
             step = ring.tile([P, S], F32, name="step")
             nc.scalar.activation(step[:], gap[:], ACT.Relu, scale=sense)
-            turned[bank] = psum.tile([P, NBLK, P], F32, name=f"turn{bank}")
+            in_bank[bank] = psum.tile([P, NBLK, P], F32, name="sum_turned", tag=f"turn{bank}")
             for i, term in enumerate((base, step)):
-                for k in range(NBLK):
+                for b in range(NBLK):
                     nc.tensor.matmul(
-                        turned[bank][:, k, :],
-                        lhsT=term[:, k * BLK : (k + 1) * BLK],
+                        in_bank[bank][:, b, :],
+                        lhsT=term[:, b * BLK : (b + 1) * BLK],
                         rhs=ident[:],
                         is_transpose=True,
-                        start=(i == 0 and k == 0),
-                        stop=(i == 1 and k == NBLK - 1),
+                        start=(i == 0 and b == 0),
+                        stop=(i == 1 and b == NBLK - 1),
                     )
 
-        def middle(bank):
-            mid = ring.tile([P, NBLK, P], F32, name="mid")
-            nc.scalar.copy(mid[:], turned[bank][:])
-            turned[bank] = psum.tile([P, NBLK, BLK], F32, name=f"turn{bank}")
-            for k in range(NBLK):
-                nc.tensor.transpose(turned[bank][:, k, :], mid[:, k, :], ident[:])
+        def turn_back(bank):
+            staged = ring.tile([P, NBLK, P], F32, name="staged")
+            nc.scalar.copy(staged[:], in_bank[bank][:])
+            in_bank[bank] = psum.tile([P, NBLK, BLK], F32, name="sum_back", tag=f"turn{bank}")
+            for b in range(NBLK):
+                nc.tensor.transpose(in_bank[bank][:, b, :], staged[:, b, :], ident[:])
 
         def land(bank, dst, sense):
-            nc.scalar.activation(dst, turned[bank][:].rearrange("p k j -> p (k j)"), ACT.Copy, scale=sense)
+            nc.scalar.activation(dst, in_bank[bank][:].rearrange("p b j -> p (b j)"), ACT.Copy, scale=sense)
 
-        def fetch4(t, lo_c, hi_c):
-            g4[t, lo_c] = keep.tile([P, hi_c - lo_c], F32, name=f"g4_{t}_{lo_c}")
-            nc.vector.tensor_copy(g4[t, lo_c][:], wide_st[t][:].indirect(n4_l[:, lo_c // PER_COL : hi_c // PER_COL]))
+        def fetch_n4(t, lo_c, hi_c):
+            by_n4[t, lo_c] = keep.tile([P, hi_c - lo_c], F32, name=f"by_n4_{t}_{lo_c}")
+            nc.vector.tensor_copy(by_n4[t, lo_c][:], st_wide[t][:].indirect(entries(n4_l, lo_c, hi_c)))
 
         def smaller(t, lo_c, hi_c):
             res = keep.tile([P, hi_c - lo_c], F32, name=f"res{t}_{lo_c}")
-            nc.vector.tensor_tensor(res[:], wide_st[t][:, lo_c:hi_c], g4[t, lo_c][:], ALU.min)
+            nc.vector.tensor_tensor(res[:], st_wide[t][:, lo_c:hi_c], by_n4[t, lo_c][:], ALU.min)
             nc.sync.dma_start(out_rows[:, t, lo_c:hi_c], res[:])
-
-        def fetch3(t):
-            g3[t] = keep.tile([P, S], F32, name=f"d3_{t}")
-            nc.vector.tensor_copy(g3[t][:], wide_a[t][:].indirect(n3_l[:]))
-
-        def larger(t):
-            nc.vector.tensor_tensor(wide_st[t][:, 0:S], wide_a[t][:, 0:S], g3[t][:], ALU.max)
 
         score_out(0, 0, PE_COLS)
         quantize_and_score(PE_BLKS)
         score_out(0, PE_COLS, S)
-        for t in (2, 3, 1):
+        for t in SCORE_ORDER[1:]:
             score_out(t, 0, S)
-        fetch3(0)
-        diff3(2)
+
+        fetch_n3(0)
+        diff_n3(2)
         larger(0)
-        diff3(3)
-        turn(0, plain[2], g3[2], 1.0)
-        neg = keep.tile([P, S], F32, name="neg")
-        nc.scalar.activation(neg[:], wide_st[0][:, 0:S], ACT.Copy, scale=-1.0)
-        middle(0)
-        turn(1, plain[3], g3[3], 1.0)
-        land(0, wide_st[2][:, 0:S], 1.0)
-        middle(1)
-        land(1, wide_st[3][:, 0:S], 1.0)
-        fetch3(1)
-        gap4 = keep.tile([P, S], F32, name="gap4")
-        nc.vector.tensor_tensor(gap4[:], wide_st[0][:].indirect(n4_l[:]), neg[:], ALU.add)
+        diff_n3(3)
+        sum_turned(0, s_plain[2], by_n3[2], 1.0)
+        st_neg = keep.tile([P, S], F32, name="st_neg")
+        nc.scalar.activation(st_neg[:], st_wide[0][:, 0:S], ACT.Copy, scale=-1.0)
+        turn_back(0)
+        sum_turned(1, s_plain[3], by_n3[3], 1.0)
+        land(0, st_wide[2][:, 0:S], 1.0)
+        turn_back(1)
+        land(1, st_wide[3][:, 0:S], 1.0)
+        fetch_n3(1)
+        st_gap = keep.tile([P, S], F32, name="st_gap")
+        nc.vector.tensor_tensor(st_gap[:], st_wide[0][:].indirect(n4_l[:]), st_neg[:], ALU.add)
         larger(1)
-        turn(2, neg, gap4, -1.0)
-        middle(2)
-        res0 = keep.tile([P, S], F32, name="res0")
-        land(2, res0[:], -1.0)
-        nc.sync.dma_start(out_rows[:, 0, :], res0[:])
-        fetch4(1, 0, S)
-        fetch4(2, 0, S)
+        sum_turned(2, st_neg, st_gap, -1.0)
+        turn_back(2)
+        res_first = keep.tile([P, S], F32, name="res_first")
+        land(2, res_first[:], -1.0)
+        nc.sync.dma_start(out_rows[:, 0, :], res_first[:])
+
+        fetch_n4(1, 0, S)
+        fetch_n4(2, 0, S)
         smaller(1, 0, S)
-        fetch4(3, 0, S // 2)
+        fetch_n4(3, *halves[0])
         smaller(2, 0, S)
-        fetch4(3, S // 2, S)
-        smaller(3, 0, S // 2)
-        smaller(3, S // 2, S)
+        fetch_n4(3, *halves[1])
+        smaller(3, *halves[0])
+        smaller(3, *halves[1])

from contextlib import ExitStack

import concourse.mybir as mybir
from concourse.masks import make_identity

K, T, S, H, C = 512, 2048, 512, 512, 512
FLOPS = 2 * K * H * S + 2 * K * C * S

F32 = mybir.dt.float32
BF16 = mybir.dt.bfloat16
I32 = mybir.dt.int32
U32 = mybir.dt.uint32
U16 = mybir.dt.uint16
U8 = mybir.dt.uint8
FP8X4 = mybir.dt.float8_e4m3fn_x4
ALU = mybir.AluOpType
ACT = mybir.ActivationFunctionType

P = 128
PACK = 4
SCALE_ROWS = K // 32
BLOCK_PARTS = P // SCALE_ROWS
QUADRANT = 32
PER_COL = 16
BLK = 128
NBLK = S // BLK
PE_BLKS = NBLK - 1
PE_COLS = PE_BLKS * BLK
WIDE = 2 * S
SCORE_SCALE = 0.0625
PE_MAX_TILES = (2, 3)
SCORE_ORDER = (0, 2, 3, 1)


def tile_picked_hcandrangehopmn_none_p_kernel(
    tc, x_words, x_scales, w1, gs, offs, n1, n2, cand, n3, n4, out
):
    nc = tc.nc
    with ExitStack() as ctx:
        keep = ctx.enter_context(tc.tile_pool(name="keep", bufs=1))
        ring = ctx.enter_context(tc.tile_pool(name="ring", bufs=2))
        psum = ctx.enter_context(tc.psum_pool(name="psum", bufs=1))

        def list_tile(name):
            return keep.tile([P, S // PER_COL], U16, name=name)

        def entries(lst, lo_c, hi_c):
            return lst[:, lo_c // PER_COL : hi_c // PER_COL]

        offs_l, cand_l = list_tile("offs_l"), list_tile("cand_l")
        n1_l, n2_l, n3_l, n4_l = (list_tile(n) for n in ("n1_l", "n2_l", "n3_l", "n4_l"))
        halves = ((0, S // 2), (S // 2, S))

        table_bytes = keep.tile([P, T], U8, name="table_bytes", align_bytes=64)
        table_words = keep.tile([P, T], I32, name="table_words", align_bytes=64)
        gs_t = keep.tile([P, PACK], F32, name="gs_t")
        w_raw = [keep.tile([P, PACK, H // 2], F32, name=f"w_raw{h}") for h in range(2)]

        w_rows = w1.rearrange("(p j) c -> p j c", j=PACK)
        nc.sync.dma_start(
            table_bytes[:].bitcast(I32),
            x_scales[0].bitcast(I32).unsqueeze(1).to_broadcast([SCALE_ROWS, BLOCK_PARTS, T // 4]),
        )
        nc.sync.dma_start(offs_l[:], offs)
        nc.sync.dma_start(cand_l[:], cand)
        nc.sync.dma_start(w_raw[0][:], w_rows[:, :, 0 : H // 2])
        nc.sync.dma_start(w_raw[1][:], w_rows[:, :, H // 2 : H])
        nc.sync.dma_start(table_words[:], x_words[0].rearrange("p c r -> p (c r)").bitcast(I32))

        x_plane = keep.tile([P, S], U8, name="x_plane", align_bytes=64)
        c_plane = keep.tile([P, C], U8, name="c_plane", align_bytes=64)
        ident = keep.tile([P, P], F32, name="ident")
        wide = [keep.tile([P, WIDE], F32, name=f"wide{t}") for t in range(PACK + 1)]
        nc.gpsimd.memset(wide[PACK][:, S:], 0.0)
        nc.gpsimd.memset(x_plane[:].bitcast(I32), 0)
        nc.gpsimd.memset(c_plane[:].bitcast(I32), 0)
        make_identity(nc, ident[:])
        nc.scalar.activation(wide[0][:, S:], wide[PACK][:, S:], ACT.Copy)

        def place_scale_rows(plane, picked):
            for b in range(QUADRANT // BLOCK_PARTS):
                nc.sync.dma_start(
                    plane[b:P:QUADRANT, :].bitcast(I32), picked[BLOCK_PARTS * b : P : QUADRANT, :].bitcast(I32)
                )

        def deal(dealt, picked):
            nc.vector.tensor_copy(
                dealt[:].rearrange("p (t m) -> p m t", t=PACK), picked[:].rearrange("p (m t) -> p m t", t=PACK)
            )

        x_bytes = keep.tile([P, S], U8, name="x_bytes", align_bytes=64)
        nc.vector.tensor_copy(x_bytes[:], table_bytes[:].indirect(offs_l[:]))
        place_scale_rows(x_plane, x_bytes)
        nc.sync.dma_start(gs_t[:], gs.rearrange("(p t) o -> p (t o)", t=PACK))
        nc.sync.dma_start(n1_l[:], n1)
        nc.sync.dma_start(n2_l[:], n2)
        nc.sync.dma_start(n3_l[:], n3)
        nc.sync.dma_start(n4_l[:], n4)

        c_bytes = keep.tile([P, C], U8, name="c_bytes", align_bytes=64)
        nc.vector.tensor_copy(c_bytes[:], table_bytes[:].indirect(cand_l[:]))
        c_bytes_dealt = keep.tile([P, C], U8, name="c_bytes_dealt", align_bytes=64)
        deal(c_bytes_dealt, c_bytes)
        place_scale_rows(c_plane, c_bytes_dealt)

        w_bf = keep.tile([P, PACK * H], BF16, name="w_bf", tag="w_bf", align_bytes=64)
        w_codes = keep.tile([P, H], U32, name="w_codes", align_bytes=64)
        w_plane = keep.tile([P, H], U8, name="w_plane", align_bytes=64)
        w_dst = w_bf[:].rearrange("p (t m j) -> p m j t", t=PACK, j=PACK)
        nc.scalar.activation(w_dst[:, 0 : P // 2], w_raw[0][:].rearrange("p j (m t) -> p m j t", t=PACK), ACT.Copy)
        nc.vector.tensor_copy(w_dst[:, P // 2 : P], w_raw[1][:].rearrange("p j (m t) -> p m j t", t=PACK))
        nc.vector.quantize_mx(out=w_codes[:].bitcast(FP8X4), scales=w_plane[:], in_=w_bf[:])

        gs_sign = keep.tile([P, PACK], F32, name="gs_sign")
        hi_weight = keep.tile([P, PACK], F32, name="hi_weight")
        lo_weight = keep.tile([P, PACK], F32, name="lo_weight")
        nc.scalar.activation(gs_sign[:], gs_t[:], ACT.Sign)
        nc.scalar.activation(hi_weight[:], gs_sign[:], ACT.Copy, scale=1.5, bias=0.5)
        nc.scalar.activation(lo_weight[:], gs_sign[:], ACT.Copy, scale=-1.5, bias=0.5)

        for t in range(1, PACK):
            nc.scalar.activation(wide[t][:, S:], wide[PACK][:, S:], ACT.Copy)

        x_codes = keep.tile([P, S], U32, name="x_codes", tag="w_bf", align_bytes=64)
        for lo_c, hi_c in halves:
            nc.vector.tensor_copy(
                x_codes[:, lo_c:hi_c], table_words[:].bitcast(U32).indirect(entries(offs_l, lo_c, hi_c))
            )

        v_plain = [keep.tile([P, S], F32, name=f"v_plain{t}") for t in range(PACK)]
        for t in range(PACK):
            rows = slice(t * P, (t + 1) * P)
            parts = zip(halves, ("acc0", "acc_half")) if t == 0 else [((0, S), f"acc{t}")]
            for (lo_c, hi_c), bank in parts:
                y_acc = psum.tile([P, hi_c - lo_c], F32, name="y_acc", tag=bank)
                nc.tensor.matmul_mx(
                    out=y_acc[:],
                    lhsT=w_codes[:, rows].bitcast(FP8X4),
                    lhsT_scale=w_plane[:, rows],
                    rhs=x_codes[:, lo_c:hi_c].bitcast(FP8X4),
                    rhs_scale=x_plane[:, lo_c:hi_c],
                    start=True,
                    stop=True,
                )
                for dst in (wide[t], v_plain[t]):
                    nc.scalar.activation(dst[:, lo_c:hi_c], y_acc[:], ACT.Copy, scale=gs_t[:, t : t + 1])

        c_words = keep.tile([P, C], U32, name="c_words", align_bytes=64)
        nc.vector.tensor_copy(c_words[:], table_words[:].bitcast(U32).indirect(cand_l[:]))
        c_codes = keep.tile([P, C], U32, name="c_codes", align_bytes=64)
        deal(c_codes, c_words)

        z_sums = [psum.tile([P, PACK, P], F32, name="z_sums", tag=f"turn{b}") for b in range(PE_BLKS)]
        z_turned = [keep.tile([P, 2, P, 2], BF16, name=f"z_turned{b}", align_bytes=64) for b in range(PE_BLKS)]

        def lead_diff(t, lst, tag):
            d = ring.tile([P, PE_COLS], F32, name="d", tag=tag)
            nc.vector.tensor_tensor(
                d[:], wide[t][:].indirect(entries(lst, 0, PE_COLS)), v_plain[t][:, 0:PE_COLS], ALU.subtract
            )
            return d

        def last_diff(d, t, lst):
            nc.vector.tensor_tensor(
                d[:, t, :], v_plain[t][:].indirect(entries(lst, PE_COLS, S)), wide[t][:, PE_COLS:S], ALU.subtract
            )

        def lead_sum(t, d1, d2):
            hi = ring.tile([P, PE_COLS], F32, name="hi")
            lo = ring.tile([P, PE_COLS], F32, name="lo")
            nc.vector.scalar_tensor_tensor(hi[:], d1[:], 0.0, d2[:], ALU.max, ALU.max)
            nc.vector.scalar_tensor_tensor(lo[:], d1[:], 0.0, d2[:], ALU.min, ALU.min)
            hi_term = ring.tile([P, PE_COLS], F32, name="hi_term")
            lo_term = ring.tile([P, PE_COLS], F32, name="lo_term")
            nc.scalar.activation(hi_term[:], hi[:], ACT.Copy, scale=hi_weight[:, t : t + 1])
            nc.scalar.activation(lo_term[:], lo[:], ACT.Copy, scale=lo_weight[:, t : t + 1])
            terms = (v_plain[t], hi_term, lo_term)
            for i, term in enumerate(terms):
                for b in range(PE_BLKS):
                    nc.tensor.matmul(
                        z_sums[b][:, t, :],
                        lhsT=term[:, b * BLK : (b + 1) * BLK],
                        rhs=ident[:],
                        is_transpose=True,
                        start=(i == 0),
                        stop=(i == len(terms) - 1),
                    )
            if t % 2 == 1:
                u = t // 2
                for b in range(PE_BLKS):
                    nc.scalar.activation(
                        z_turned[b][:, u],
                        z_sums[b][:, 2 * u : 2 * u + 2, :].rearrange("j e p -> j p e"),
                        ACT.Copy,
                        scale=0.5,
                    )

        d1_next = lead_diff(0, n1_l, "d1")
        for t in range(PACK):
            d1_now = d1_next
            d2_now = lead_diff(t, n2_l, "d2")
            if t + 1 < PACK:
                d1_next = lead_diff(t + 1, n1_l, "d1")
            else:
                d1_last = ring.tile([P, PACK, BLK], F32, name="d1_last", tag="d1")
                last_diff(d1_last, 0, n1_l)
            lead_sum(t, d1_now, d2_now)

        z_bf = [keep.tile([P, BLK * PACK], BF16, name="z_bf", tag=f"z_bf{b}", align_bytes=64) for b in range(PE_BLKS)]
        z_codes = [keep.tile([P, BLK], U32, name=f"z_codes{b}", align_bytes=64) for b in range(NBLK)]
        z_plane = [keep.tile([P, BLK], U8, name=f"z_plane{b}", align_bytes=64) for b in range(NBLK)]
        for b in range(PE_BLKS):
            z_pairs = psum.tile([P, 2, BLK], F32, name="z_pairs", tag=f"turn{b}")
            pair_words = z_turned[b][:].rearrange("j u p e -> j (u p e)").bitcast(F32)
            for u in range(2):
                nc.tensor.transpose(z_pairs[:, u, :], pair_words[:, u * P : (u + 1) * P], ident[:])
            nc.scalar.copy(
                z_bf[b][:].bitcast(F32).rearrange("p (j u) -> p j u", u=2), z_pairs[:].rearrange("p u j -> p j u")
            )

        s_acc = [psum.tile([P, S], F32, name="s_acc", tag=f"acc{t}") for t in range(PACK)]

        def quantize_and_score(b):
            nc.vector.quantize_mx(out=z_codes[b][:].bitcast(FP8X4), scales=z_plane[b][:], in_=z_bf[b][:])
            for t in SCORE_ORDER:
                rows = slice(t * P, (t + 1) * P)
                nc.tensor.matmul_mx(
                    out=s_acc[t][:, b * BLK : (b + 1) * BLK],
                    lhsT=c_codes[:, rows].bitcast(FP8X4),
                    lhsT_scale=c_plane[:, rows],
                    rhs=z_codes[b][:].bitcast(FP8X4),
                    rhs_scale=z_plane[b][:],
                    start=True,
                    stop=True,
                )

        d2_last = ring.tile([P, PACK, BLK], F32, name="d2_last", tag="d2")
        for t in range(PACK):
            if t > 0:
                last_diff(d1_last, t, n1_l)
            last_diff(d2_last, t, n2_l)
        hi_last = keep.tile([P, PACK, BLK], F32, name="hi_last")
        lo_last = keep.tile([P, PACK, BLK], F32, name="lo_last")
        nc.vector.scalar_tensor_tensor(hi_last[:], d1_last[:], 0.0, d2_last[:], ALU.max, ALU.max)
        nc.vector.scalar_tensor_tensor(lo_last[:], d1_last[:], 0.0, d2_last[:], ALU.min, ALU.min)
        z_part = keep.tile([P, PACK, BLK], F32, name="z_part")
        for t in range(PACK):
            nc.vector.scalar_tensor_tensor(
                z_part[:, t, :], hi_last[:, t, :], hi_weight[:, t : t + 1], v_plain[t][:, PE_COLS:S], ALU.mult, ALU.add
            )
        quantize_and_score(0)
        quantize_and_score(1)
        z_twice = keep.tile([P, PACK, BLK], F32, name="z_twice", tag="z_bf1", align_bytes=64)
        for t in range(PACK):
            nc.vector.scalar_tensor_tensor(
                z_twice[:, t, :], lo_last[:, t, :], lo_weight[:, t : t + 1], z_part[:, t, :], ALU.mult, ALU.add
            )
        quantize_and_score(2)
        z_bf.append(keep.tile([P, BLK * PACK], BF16, name="z_bf_last", tag="z_bf2", align_bytes=64))
        nc.vector.tensor_scalar(
            z_bf[PE_BLKS][:].rearrange("p (c i t) -> p c t i", i=4, t=PACK),
            z_twice[:].rearrange("p t (c i) -> p c t i", i=4),
            0.5,
            None,
            ALU.mult,
        )

        out_rows = out.rearrange("(p t) j -> p t j", t=PACK)
        s_plain = {t: keep.tile([P, S], F32, name=f"s_plain{t}") for t in PE_MAX_TILES}
        st_wide = [wide[2], wide[PACK], wide[0], wide[3]]
        by_n3, by_n4, in_bank = {}, {}, {}

        def score_out(t, lo_c, hi_c):
            nc.scalar.activation(wide[t][:, lo_c:hi_c], s_acc[t][:, lo_c:hi_c], ACT.Copy, scale=SCORE_SCALE)
            if t in s_plain:
                nc.scalar.activation(s_plain[t][:, lo_c:hi_c], s_acc[t][:, lo_c:hi_c], ACT.Copy, scale=SCORE_SCALE)

        def fetch_n3(t):
            by_n3[t] = keep.tile([P, S], F32, name=f"by_n3_{t}")
            nc.vector.tensor_copy(by_n3[t][:], wide[t][:].indirect(n3_l[:]))

        def diff_n3(t):
            by_n3[t] = keep.tile([P, S], F32, name=f"by_n3_{t}")
            nc.vector.tensor_tensor(by_n3[t][:], wide[t][:].indirect(n3_l[:]), s_plain[t][:], ALU.subtract)

        def larger(t):
            nc.vector.tensor_tensor(st_wide[t][:, 0:S], wide[t][:, 0:S], by_n3[t][:], ALU.max)

        def sum_turned(bank, base, gap, sense):
            step = ring.tile([P, S], F32, name="step")
            nc.scalar.activation(step[:], gap[:], ACT.Relu, scale=sense)
            in_bank[bank] = psum.tile([P, NBLK, P], F32, name="sum_turned", tag=f"turn{bank}")
            for i, term in enumerate((base, step)):
                for b in range(NBLK):
                    nc.tensor.matmul(
                        in_bank[bank][:, b, :],
                        lhsT=term[:, b * BLK : (b + 1) * BLK],
                        rhs=ident[:],
                        is_transpose=True,
                        start=(i == 0 and b == 0),
                        stop=(i == 1 and b == NBLK - 1),
                    )

        def turn_back(bank):
            staged = ring.tile([P, NBLK, P], F32, name="staged")
            nc.scalar.copy(staged[:], in_bank[bank][:])
            in_bank[bank] = psum.tile([P, NBLK, BLK], F32, name="sum_back", tag=f"turn{bank}")
            for b in range(NBLK):
                nc.tensor.transpose(in_bank[bank][:, b, :], staged[:, b, :], ident[:])

        def land(bank, dst, sense):
            nc.scalar.activation(dst, in_bank[bank][:].rearrange("p b j -> p (b j)"), ACT.Copy, scale=sense)

        def fetch_n4(t, lo_c, hi_c):
            by_n4[t, lo_c] = keep.tile([P, hi_c - lo_c], F32, name=f"by_n4_{t}_{lo_c}")
            nc.vector.tensor_copy(by_n4[t, lo_c][:], st_wide[t][:].indirect(entries(n4_l, lo_c, hi_c)))

        def smaller(t, lo_c, hi_c):
            res = keep.tile([P, hi_c - lo_c], F32, name=f"res{t}_{lo_c}")
            nc.vector.tensor_tensor(res[:], st_wide[t][:, lo_c:hi_c], by_n4[t, lo_c][:], ALU.min)
            nc.sync.dma_start(out_rows[:, t, lo_c:hi_c], res[:])

        score_out(0, 0, PE_COLS)
        quantize_and_score(PE_BLKS)
        score_out(0, PE_COLS, S)
        for t in SCORE_ORDER[1:]:
            score_out(t, 0, S)

        fetch_n3(0)
        diff_n3(2)
        larger(0)
        diff_n3(3)
        sum_turned(0, s_plain[2], by_n3[2], 1.0)
        st_neg = keep.tile([P, S], F32, name="st_neg")
        nc.scalar.activation(st_neg[:], st_wide[0][:, 0:S], ACT.Copy, scale=-1.0)
        turn_back(0)
        sum_turned(1, s_plain[3], by_n3[3], 1.0)
        land(0, st_wide[2][:, 0:S], 1.0)
        turn_back(1)
        land(1, st_wide[3][:, 0:S], 1.0)
        fetch_n3(1)
        st_gap = keep.tile([P, S], F32, name="st_gap")
        nc.vector.tensor_tensor(st_gap[:], st_wide[0][:].indirect(n4_l[:]), st_neg[:], ALU.add)
        larger(1)
        sum_turned(2, st_neg, st_gap, -1.0)
        turn_back(2)
        res_first = keep.tile([P, S], F32, name="res_first")
        land(2, res_first[:], -1.0)
        nc.sync.dma_start(out_rows[:, 0, :], res_first[:])

        fetch_n4(1, 0, S)
        fetch_n4(2, 0, S)
        smaller(1, 0, S)
        fetch_n4(3, *halves[0])
        smaller(2, 0, S)
        fetch_n4(3, *halves[1])
        smaller(3, *halves[0])
        smaller(3, *halves[1])
